import numpy as np
CORES = [67,68,75,76,83,84,91,92,99,100,107,108,115,116,123,124]
N = 16
def setup_inputs(rng):
    return {"x": rng.standard_normal((N, 128, 256), dtype=np.float32)}
def reference(x):
    g = np.concatenate(list(x), axis=1)
    return {"y": np.broadcast_to(g, (N,) + g.shape)}

from concourse.bass import DstId, RemoteDMATransfer

W = 256
H = W // 2
NPAIR = 4
FIRST_CHIP = 8
A_CORE, B_CORE = 3, 4
OFF = 0x00FF
OFF_LO, OFF_HI = 0x000F, 0x00F0
ON = 0xFF00
ALL = 0xFFFF

SCRATCH = {
    "land": ("sbuf", [128, 16 * W], "float32"),
}
SEMAPHORES = ["ld", "st", "sent"] + ["s_%d" % r for r in range(16)]


def chip_of(k, parity):
    return FIRST_CHIP + 2 * (k % NPAIR) + parity


def plan():
    calls = []

    def core(c, i):
        return 8 * c + i

    def both(c):
        return [core(c, A_CORE), core(c, B_CORE)]

    for s in range(FIRST_CHIP, FIRST_CHIP + 2 * NPAIR):
        k, par = (s - FIRST_CHIP) // 2, s & 1
        m = s ^ 1
        P = [chip_of(k + j, par) for j in range(NPAIR)]
        Q = [chip_of(k + j, 1 - par) for j in range(NPAIR)]
        a = 2 * (s - FIRST_CHIP)
        b = a + 1

        calls.append((1, 0, core(s, A_CORE), a, [(0, H, [core(m, 1)], OFF_LO), (H, W, [core(m, 6)], OFF_HI)]))
        calls.append((1, 1, core(s, A_CORE), a, [(0, W, [core(P[1], 2), core(P[2], 0), core(P[3], 2)], OFF),
                                                 (0, W, [core(s, B_CORE)], ON)]))
        calls.append((2, 1, core(m, 1), a, [(0, H, [core(Q[2], 5)], OFF), (0, H, both(m), ON)]))
        calls.append((2, 1, core(m, 6), a, [(H, W, [core(Q[2], 5)], OFF), (H, W, both(m), ON)]))
        calls.append((3, 0, core(Q[2], 5), a, [(0, W, both(Q[2]), ALL)]))
        calls.append((2, 2, core(P[2], 0), a, [(0, W, both(P[2]), ALL)]))
        for j in (1, 3):
            calls.append((2, 1 + j, core(P[j], 2), a, [(0, W, [core(Q[j], 1)], OFF), (0, W, both(P[j]), ON)]))
            calls.append((3, 1 + j, core(Q[j], 1), a, [(0, W, both(Q[j]), ALL)]))

        calls.append((1, 0, core(s, B_CORE), b, [(H, W, [core(s, 6)], ON)]))
        calls.append((1, 1, core(s, B_CORE), b, [(0, W, [core(P[1], 7), core(P[2], 6), core(P[3], 7)], OFF),
                                                 (0, W, [core(s, A_CORE)], ON)]))
        calls.append((2, 0, core(s, A_CORE), b, [(0, H, [core(m, 0)], OFF)]))
        calls.append((2, 0, core(s, 6), b, [(H, W, [core(m, 0)], OFF)]))
        calls.append((3, 0, core(m, 0), b, [(0, W, both(m), ALL)]))
        calls.append((2, 3, core(P[2], 6), b, [(0, W, [core(Q[2], 0)], OFF), (0, W, both(P[2]), ON)]))
        calls.append((3, 3, core(Q[2], 0), b, [(0, W, both(Q[2]), ALL)]))
        for j in (1, 3):
            calls.append((2, 1 + j, core(P[j], 7), b, [(0, W, [core(Q[j], 5)], OFF), (0, W, both(P[j]), ON)]))
            calls.append((3, 1 + j, core(Q[j], 5), b, [(0, W, both(Q[j]), ALL)]))
    return calls


def engines(mask):
    return bin(mask).count("1")


def rank_program(g, core, T, topo):
    chip = topo.chip(core)
    if chip < FIRST_CHIP:
        return
    calls = plan()
    rank = T.rank_of(core)

    full = {}
    for _hop, _turn, _snd, r, parts in calls:
        for _lo, _hi, dsts, mask in parts:
            if core in dsts:
                full[r] = full.get(r, 0) + engines(mask)

    def wait_block(q, r):
        if r == rank:
            q.wait_ge(T.sem.ld, 16)
        else:
            q.wait_ge(T.sem["s_%d" % r], full[r])

    def did(c):
        rid, pid, _se = topo.addr(c)
        return DstId(rid=rid, pnc=pid)

    if rank is not None:
        g.sync.dma_start(T.land[:, rank * W:(rank + 1) * W], T.x[:]).then_inc(T.sem.ld, 16)

    sent = 0
    mine = sorted([c for c in calls if c[2] == core], key=lambda c: (c[0], c[1]))
    for _hop, _turn, _snd, r, parts in mine:
        wait_block(g, r)
        transfers = []
        for lo, hi, dsts, mask in parts:
            ap = T.land[:, r * W + lo:r * W + hi]
            transfers.append(RemoteDMATransfer(dst_ids=[did(d) for d in dsts], dma_engine_mask=mask,
                                               remote_sem=T.sem["s_%d" % r], srcs=[ap], dsts=[ap for _d in dsts]))
            sent += engines(mask)
        g.remote_dma_fused(transfers, local_sem=T.sem.sent)

    if rank is not None:
        k, par = (chip - FIRST_CHIP) // 2, chip & 1
        order = [chip_of(k - j, par) for j in (0, 2, 1, 3)] + [chip_of(k - j, 1 - par) for j in (0, 2, 1, 3)]
        queues = [g.sync, g.scalar]
        for i, c in enumerate(order):
            q = queues[i % 2]
            r = 2 * (c - FIRST_CHIP)
            wait_block(q, r)
            wait_block(q, r + 1)
            q.dma_start(T.y[:, r * W:(r + 2) * W], T.land[:, r * W:(r + 2) * W]).then_inc(T.sem.st, 16)
        g.wait_ge(T.sem.st, 16 * len(order))

    g.wait_ge(T.sem.sent, sent)
